import numpy as np
import ml_dtypes


def mxq(x, axis, fmt="e4m3"):
    dtype, down = {"e4m3": (ml_dtypes.float8_e4m3fn, 7), "e5m2": (ml_dtypes.float8_e5m2, 14)}[fmt]
    v = np.moveaxis(np.asarray(x, np.float32).astype(ml_dtypes.bfloat16).astype(np.float64), axis, -1)
    blocks = v.reshape(v.shape[:-1] + (-1, 32))
    amax = np.abs(blocks).max(-1, keepdims=True)
    byte = np.maximum(np.where(amax > 0, np.frexp(amax)[1] - 1 + 127, 0) - down, 1)
    scale = np.exp2(byte - 127.0)
    codes = (blocks / scale).astype(np.float32).astype(dtype).astype(np.float64)
    return np.moveaxis((codes * scale).reshape(v.shape), -1, axis)


WIDE = False


def mx_kscale(k):
    if not WIDE:
        return np.ones(k)
    levels = np.array([10, -10, 5, -5, 0])
    if k % 512:
        return np.exp2(np.random.permutation(np.resize(levels, k // 32))).repeat(32)
    a = np.empty((k // 512, 16))
    for p in range(k // 512):
        a[p, :8] = np.random.permutation(np.resize(levels, 8))
        for g in range(8):
            far = levels[np.abs(levels - a[p, g]) >= 10]
            a[p, g + 8] = far[np.random.randint(len(far))]
    return np.exp2(a.ravel()).repeat(32)


def f64(x):
    return np.asarray(x).astype(np.float64)


def striped(idx):
    return np.tile(idx.reshape(-1, 16).T, (8, 1)).astype(np.uint16)


def unstriped(offs):
    return offs[:16].T.reshape(-1).astype(np.int64)


E2M1 = np.array([0.0, 0.5, 1.0, 1.5, 2.0, 3.0, 4.0, 6.0, -0.0, -0.5, -1.0, -1.5, -2.0, -3.0, -4.0, -6.0])


def pack_weight(w, fmt):
    k, n = w.shape
    w = f64(np.asarray(w, np.float32).astype(ml_dtypes.bfloat16)).reshape(k // 32, 32, n)
    amax = np.abs(w).max(1)
    if fmt == "e4m3":
        byte = np.frexp(amax)[1] - 1 + 127 - 7
    else:
        mant, ex = np.frexp(amax / 6.0)
        byte = np.where(mant > 0.5, ex, ex - 1) + 127
    byte = np.clip(np.where(amax > 0, byte, 1), 1, 254)
    scaled = (w * np.exp2(127.0 - byte)[:, None, :]).reshape(k, n).astype(np.float32)
    by_word = np.ascontiguousarray(scaled.reshape(k // 512, 128, 4, n).transpose(0, 1, 3, 2))
    if fmt == "e4m3":
        words = by_word.astype(ml_dtypes.float8_e4m3fn).view(np.uint8)
    else:
        c = by_word.astype(ml_dtypes.float4_e2m1fn).view(np.uint8) & 0xF
        words = (c[..., 0::2] | (c[..., 1::2] << 4)).reshape(k // 512, 128, 2 * n)
    return np.ascontiguousarray(words), np.ascontiguousarray(byte.astype(np.uint8).reshape(k // 512, 16, n))


def unpack_weight(words, scales, fmt):
    g, _, n = scales.shape
    words = np.ascontiguousarray(words).reshape(g, 128, n, -1)
    if fmt == "e4m3":
        vals = words.view(ml_dtypes.float8_e4m3fn).astype(np.float64)
    else:
        nib = np.empty((g, 128, n, 4), np.uint8)
        nib[..., 0::2] = words & 0xF
        nib[..., 1::2] = words >> 4
        vals = E2M1[nib]
    vals = vals * np.repeat(np.exp2(scales.astype(np.float64) - 127.0), 8, axis=1)[..., None]
    return vals.transpose(0, 1, 3, 2).reshape(g * 512, n)


def gelu(v):
    return 0.5 * v * (1.0 + np.tanh(np.sqrt(2.0 / np.pi) * (v + 0.044715 * v**3)))


def striped8(idx):
    return np.concatenate([v.reshape(-1, 16).T for v in idx]).astype(np.uint16)


def unstriped8(offs):
    return np.stack([offs[16 * g:16 * g + 16].T.reshape(-1) for g in range(8)]).astype(np.int64)


def heads(h, wgt, idx8):
    r = np.arange(h.shape[0])
    return wgt[r // 4 % 128] * h[r[:, None], idx8[r % 512 // 64]]


def put_heads(h, wgs, idx8, t2):
    r = np.arange(h.shape[0])
    page = np.zeros((h.shape[0], t2))
    page[r[:, None], idx8[r % 512 // 64]] = wgs[r // 4 % 128] * h
    return page


K, H, T, S, P, T2 = 1536, 1024, 4096, 1024, 512, 1024

def setup_inputs():
    n = np.random.standard_normal
    s = mx_kscale(K)[:, None]
    u = mx_kscale(H)[:, None]
    d = {}
    d["tab_words"], d["tab_scales"] = pack_weight(n((K, T)) * s, "e4m3")
    d["offs"] = striped(np.random.permutation(T)[:S])
    d["w1"] = (n((K, H)) / K**0.5 / s).astype(np.float32)
    d["gain"] = (np.exp(0.3 * n(H)) * u[:, 0]).astype(np.float32)
    d["offs2"] = striped8(np.stack([np.random.permutation(S)[:P] for _ in range(8)]))
    d["wgt"] = np.repeat(np.random.uniform(0.5, 2.0, (8, P)), 16, axis=0).astype(np.float32)
    d["blank"] = (n((H, P)) * u).astype(np.float32)
    d["w4_words"], d["w4_scales"] = pack_weight(n((H, H)) / H**0.5 / u, "e2m1")
    d["clear"] = (np.exp(0.3 * n(H)) / u[:, 0]).astype(np.float32)
    d["offs3"] = striped8(np.stack([np.random.permutation(T2)[:P] for _ in range(8)]))
    d["wgo"] = np.repeat(np.random.uniform(0.5, 2.0, (8, P)), 16, axis=0).astype(np.float32)
    return d

def reference(tab_words, tab_scales, offs, w1, gain, offs2, wgt, blank, w4_words, w4_scales, clear, offs3, wgo):
    v = unpack_weight(tab_words, tab_scales, "e4m3")[:, unstriped(offs)]
    w4 = unpack_weight(w4_words, w4_scales, "e2m1")
    h = f64(gain)[:, None] * (mxq(f64(w1), 0, "e4m3").T @ v)
    x = heads(h, f64(wgt), unstriped8(offs2))
    z = x - f64(blank)
    e = w4.T @ mxq(z, 0, "e4m3")
    y = e / (1.0 + np.abs(f64(clear)[:, None] * z))
    out = put_heads(y, f64(wgo), unstriped8(offs3), T2)
    return out

@@ -1,0 +1,288 @@
+from contextlib import ExitStack
+
+import concourse.mybir as mybir
+
+F32 = mybir.dt.float32
+BF16 = mybir.dt.bfloat16
+I32 = mybir.dt.int32
+U32 = mybir.dt.uint32
+U16 = mybir.dt.uint16
+U8 = mybir.dt.uint8
+E4M3X4 = mybir.dt.float8_e4m3fn_x4
+E2M1X4 = mybir.dt.float4_e2m1fn_x4
+ACT = mybir.ActivationFunctionType
+MULT = mybir.AluOpType.mult
+SUB = mybir.AluOpType.subtract
+
+K, H, T, S, M, T2 = 1536, 1024, 4096, 1024, 512, 1024
+FLOPS = 2 * K * H * S + 2 * H * H * M
+
+P = 128
+PACK = 4
+SPAN = P * PACK
+KP = K // SPAN
+HB = H // SPAN
+BANK = 512
+HALF = M // 2
+PAGES = 3
+SPLIT_TILES = 2
+VEC_SHARE = 88
+
+
+def tile_list_ballot_mark_doubts_kernel(
+    tc, tab_words, tab_scales, offs, w1, gain, offs2, wgt, blank, w4_words, w4_scales, clear, offs3, wgo, out
+):
+    nc = tc.nc
+    with ExitStack() as ctx:
+        keep = ctx.enter_context(tc.tile_pool(name="keep", bufs=1))
+        ring = ctx.enter_context(tc.tile_pool(name="ring", bufs=2))
+        psum = ctx.enter_context(tc.psum_pool(name="psum", bufs=8))
+
+        def kept(name, shape, dtype):
+            return keep.tile(shape, dtype, name=name, align_bytes=64)
+
+        def slab(name, shape):
+            return ring.tile(shape, F32, name=name, tag="slab", bufs=KP * HB, align_bytes=64)
+
+        offs_sb = kept("offs_sb", [P, S // 16], U16)
+        offs2_sb = kept("offs2_sb", [P, M // 16], U16)
+        offs3_sb = kept("offs3_sb", [P, M // 16], U16)
+        tab_sb = [kept("tab%d" % a, [P, T], U32) for a in range(KP)]
+        tabs_sb = kept("tabs_sb", [P, T], U8)
+        w4_raw = kept("w4_raw", [P, HB * 2 * H], U8)
+        w4s_raw = kept("w4s_raw", [P, HB * H], U8)
+        gain_sb = kept("gain_sb", [P, HB, PACK], F32)
+        clear_sb = kept("clear_sb", [P, HB, PACK], F32)
+        wgt_sb = kept("wgt_sb", [P, M], F32)
+        wgo_sb = kept("wgo_sb", [P, M], F32)
+        blank_sb = [kept("blank%d" % b, [P, PACK, M], F32) for b in range(HB)]
+        pages = [kept("page%d" % j, [P, T2], F32) for j in range(PAGES)]
+        warm = kept("warm", [P, 2], F32)
+
+        nc.vector.memset(tabs_sb[:].bitcast(I32), 0)
+        nc.vector.memset(w4s_raw[:].bitcast(I32), 0)
+        nc.vector.memset(warm[:, 0:1], 1.0)
+        nc.scalar.activation(out=warm[:, 1:2], in_=warm[:, 0:1], func=ACT.Abs_reciprocal_sqrt)
+        for page in pages:
+            nc.vector.memset(page[:], 0.0)
+
+        tabs32 = tab_scales.bitcast(I32)
+        w4s32 = w4_scales.bitcast(I32)
+
+        def load_tab_scales():
+            for q in range(4):
+                nc.sync.dma_start(
+                    out=tabs_sb[32 * q : 32 * q + 4 * KP, :].bitcast(I32), in_=tabs32[:, 4 * q : 4 * q + 4, :]
+                )
+
+        def load_w4_scales():
+            for q in range(4):
+                nc.sync.dma_start(
+                    out=w4s_raw[32 * q : 32 * q + 4, :].bitcast(I32).rearrange("r (a n) -> r a n", a=HB),
+                    in_=w4s32[:, 4 * q : 4 * q + 4, :].rearrange("a r n -> r a n"),
+                )
+
+        def load_rows_vector(dst, vec):
+            nc.sync.dma_start(out=dst[:], in_=vec.rearrange("(b p i) -> p b i", b=HB, i=PACK))
+
+        raw = {}
+
+        def load_tab(a):
+            nc.sync.dma_start(
+                out=tab_sb[a][:].bitcast(I32), in_=tab_words[a].rearrange("p n t -> p (n t)").bitcast(I32)
+            )
+
+        def load_w1(a, b):
+            raw[a, b] = slab("raw%d%d" % (a, b), [P, PACK, SPAN])
+            rows = w1[a * SPAN : (a + 1) * SPAN, b * SPAN : (b + 1) * SPAN]
+            nc.sync.dma_start(out=raw[a, b][:], in_=rows.rearrange("(p j) c -> p j c", j=PACK))
+
+        def load_blank(b):
+            rows = blank[b * SPAN : (b + 1) * SPAN, :]
+            nc.sync.dma_start(out=blank_sb[b][:], in_=rows.rearrange("(p i) m -> p i m", i=PACK))
+
+        load_tab(0)
+        load_tab_scales()
+        nc.sync.dma_start(out=offs_sb[:], in_=offs)
+        nc.sync.dma_start(
+            out=w4_raw[:].bitcast(I32).rearrange("p (a n) -> p a n", a=HB),
+            in_=w4_words.bitcast(I32).rearrange("a p n -> p a n"),
+        )
+        load_w1(0, 0)
+        load_tab(1)
+        load_w1(1, 0)
+        load_w4_scales()
+        load_rows_vector(gain_sb, gain)
+        load_tab(2)
+        load_w1(2, 0)
+        nc.sync.dma_start(out=offs2_sb[:], in_=offs2)
+        nc.sync.dma_start(out=wgt_sb[:], in_=wgt)
+        load_blank(0)
+        for a in range(KP):
+            load_w1(a, 1)
+        load_rows_vector(clear_sb, clear)
+        load_blank(1)
+        nc.sync.dma_start(out=offs3_sb[:], in_=offs3)
+        nc.sync.dma_start(out=wgo_sb[:], in_=wgo)
+
+        v_codes = [kept("v_codes%d" % a, [P, S], U32) for a in range(KP)]
+        v_scales = kept("v_scales", [P, S], U8)
+        w1_codes = {(a, b): kept("w1c%d%d" % (a, b), [P, SPAN], U32) for a in range(KP) for b in range(HB)}
+        w1_scales = {(a, b): kept("w1s%d%d" % (a, b), [P, SPAN], U8) for a in range(KP) for b in range(HB)}
+        w4_codes = kept("w4_codes", [P, HB * 2 * H], U8)
+        w4_sc = kept("w4_sc", [P, HB * H], U8)
+
+        def gather_tab(a):
+            nc.vector.tensor_copy(out=v_codes[a][:], in_=tab_sb[a][:].indirect(offs_sb[:]))
+
+        def deal_w4():
+            nc.vector.tensor_copy(
+                out=w4_codes[:].rearrange("p (g i q e) -> p g q i e", i=PACK, q=P, e=2),
+                in_=w4_raw[:].rearrange("p (g q i e) -> p g q i e", i=PACK, q=P, e=2),
+            )
+            nc.vector.tensor_copy(
+                out=w4_sc[:].rearrange("p (g i q) -> p g q i", i=PACK, q=P),
+                in_=w4s_raw[:].rearrange("p (g q i) -> p g q i", i=PACK, q=P),
+            )
+
+        def quantize_w1(a, b, vec_cols, pieces):
+            grouped = ring.tile([P, PACK * SPAN], BF16, name="grouped", align_bytes=64)
+            dst = grouped[:].rearrange("p (t q j) -> p q j t", t=PACK, j=PACK)
+            src = raw[a, b][:].rearrange("p j (q t) -> p q j t", t=PACK)
+            if vec_cols > 0:
+                nc.vector.tensor_copy(out=dst[:, :vec_cols], in_=src[:, :vec_cols])
+            if vec_cols < P:
+                nc.scalar.copy(out=dst[:, vec_cols:], in_=src[:, vec_cols:])
+            width = SPAN // pieces
+            for c in range(0, SPAN, width):
+                nc.vector.quantize_mx(
+                    out=w1_codes[a, b][:, c : c + width].bitcast(E4M3X4),
+                    scales=w1_scales[a, b][:, c : c + width],
+                    in_=grouped[:, PACK * c : PACK * (c + width)],
+                )
+
+        h_sb = {}
+
+        def first_product(b):
+            for i in range(PACK):
+                h_sb[b, i] = ring.tile([P, S], F32, name="h_sb", bufs=4, align_bytes=64)
+                cols = slice(i * P, (i + 1) * P)
+                for s in range(0, S, BANK):
+                    acc = psum.tile([P, BANK], F32, name="acc")
+                    for a in range(KP):
+                        nc.tensor.matmul_mx(
+                            out=acc[:],
+                            lhsT=w1_codes[a, b][:, cols].bitcast(E4M3X4),
+                            lhsT_scale=w1_scales[a, b][:, cols],
+                            rhs=v_codes[a][:, s : s + BANK].bitcast(E4M3X4),
+                            rhs_scale=v_scales[4 * a : P, s : s + BANK],
+                            start=(a == 0),
+                            stop=(a == KP - 1),
+                        )
+                    nc.scalar.activation(
+                        out=h_sb[b, i][:, s : s + BANK], in_=acc[:], func=ACT.Copy, scale=gain_sb[:, b, i : i + 1]
+                    )
+
+        z_codes = [kept("z_codes%d" % b, [P, M], U32) for b in range(HB)]
+        z_scales = [kept("z_scales%d" % b, [P, M], U8) for b in range(HB)]
+        z_sb = {}
+
+        def entries(lists, m0, width):
+            return lists[:, m0 // 16 : (m0 + width) // 16]
+
+        def make_z(b, m0, width):
+            z = slab("z%d_%d" % (b, m0), [P, PACK, width])
+            z_sb[b, m0] = z
+            cols = slice(m0, m0 + width)
+            for i in range(PACK + 1):
+                if i < PACK:
+                    nc.vector.tensor_tensor(
+                        out=z[:, i, :], in0=h_sb[b, i][:].indirect(entries(offs2_sb, m0, width)), in1=wgt_sb[:, cols], op=MULT
+                    )
+                if i > 0:
+                    nc.vector.tensor_tensor(
+                        out=z[:, i - 1, :], in0=z[:, i - 1, :], in1=blank_sb[b][:, i - 1, cols], op=SUB
+                    )
+
+        def quantize_z(b, m0, width):
+            zq = ring.tile([P, PACK * width], BF16, name="zq", align_bytes=64)
+            nc.scalar.copy(
+                out=zq[:].rearrange("p (c k i) -> p c i k", k=4, i=PACK),
+                in_=z_sb[b, m0][:].rearrange("p i (c k) -> p c i k", k=4),
+            )
+            nc.vector.quantize_mx(
+                out=z_codes[b][:, m0 : m0 + width].bitcast(E4M3X4), scales=z_scales[b][:, m0 : m0 + width], in_=zq[:]
+            )
+
+        damp = {}
+
+        def make_damp(b, i, m0, width):
+            r = damp[b][:, i, m0 : m0 + width]
+            for (zb, z0), z in z_sb.items():
+                lo, hi = max(m0, z0), min(m0 + width, z0 + z.shape[2])
+                if zb == b and lo < hi:
+                    nc.scalar.activation(
+                        out=damp[b][:, i, lo:hi], in_=z[:, i, lo - z0 : hi - z0], func=ACT.Abs, scale=clear_sb[:, b, i : i + 1]
+                    )
+            nc.scalar.activation(out=r, in_=r, func=ACT.Abs_reciprocal_sqrt, bias=1.0)
+            nc.scalar.activation(out=r, in_=r, func=ACT.Square)
+
+        def make_y(b, i, m0, width):
+            acc = psum.tile([P, BANK], F32, name="acc")
+            step = BANK if width == BANK else P
+            for c in range(0, width, step):
+                for a in range(HB):
+                    col = (a * HB + b) * SPAN + i * P
+                    nc.tensor.matmul_mx(
+                        out=acc[:, c : c + step],
+                        lhsT=w4_codes[:, 2 * col : 2 * (col + P)].bitcast(E2M1X4),
+                        lhsT_scale=w4_sc[:, col : col + P],
+                        rhs=z_codes[a][:, m0 + c : m0 + c + step].bitcast(E4M3X4),
+                        rhs_scale=z_scales[a][:, m0 + c : m0 + c + step],
+                        start=(a == 0),
+                        stop=(a == HB - 1),
+                    )
+            make_damp(b, i, m0, width)
+            y = ring.tile([P, M], F32, name="y", bufs=3, align_bytes=64)
+            nc.vector.tensor_tensor(out=y[:, :width], in0=acc[:, :width], in1=damp[b][:, i, m0 : m0 + width], op=MULT)
+            return y
+
+        def place(y, b, i, m0, width):
+            page = pages[(b * PACK + i) % PAGES]
+            nc.vector.tensor_tensor(
+                out=page[:].indirect(entries(offs3_sb, m0, width)), in0=y[:, :width], in1=wgo_sb[:, m0 : m0 + width], op=MULT
+            )
+            if m0 + width == M:
+                rows = out[b * SPAN : (b + 1) * SPAN, :].rearrange("(p i) n -> p i n", i=PACK)
+                nc.sync.dma_start(out=rows[:, i, :], in_=page[:])
+
+        gather_tab(0)
+        nc.vector.tensor_copy(out=v_scales[:], in_=tabs_sb[:].indirect(offs_sb[:]))
+        quantize_w1(0, 0, 0, 1)
+        deal_w4()
+        gather_tab(1)
+        quantize_w1(1, 0, 0, 1)
+        gather_tab(2)
+        quantize_w1(2, 0, VEC_SHARE, PACK)
+        first_product(0)
+        make_z(0, 0, M)
+        quantize_w1(0, 1, 0, 1)
+        quantize_w1(1, 1, 0, 1)
+        quantize_w1(2, 1, P, PACK)
+        quantize_z(0, 0, M)
+        first_product(1)
+        make_z(1, 0, HALF)
+        quantize_z(1, 0, HALF)
+        make_z(1, HALF, HALF)
+        quantize_z(1, HALF, HALF)
+
+        for b in range(HB):
+            damp[b] = slab("damp%d" % b, [P, PACK, M])
+        steps = [(0, i, m0, HALF) for m0 in (0, HALF) for i in range(SPLIT_TILES)]
+        steps = steps + [(n // PACK, n % PACK, 0, M) for n in range(SPLIT_TILES, HB * PACK)]
+        ahead = make_y(*steps[0])
+        for n, step in enumerate(steps):
+            y = ahead
+            if n + 1 < len(steps):
+                ahead = make_y(*steps[n + 1])
+            place(y, *step)

@@ -1,6 +1,7 @@
 from contextlib import ExitStack
 
 import concourse.mybir as mybir
+from concourse.masks import make_identity
 
 F32 = mybir.dt.float32
 BF16 = mybir.dt.bfloat16
@@ -24,8 +25,11 @@ KP = K // SPAN
 HB = H // SPAN
 BANK = 512
 HALF = M // 2
-PAGES = 3
-SPLIT_TILES = 2
+GROUPS = 8
+GROUP_ROWS = P // GROUPS
+M_BLOCKS = M // P
+PAGES = 8
+SPLIT_TILES = 3
 VEC_SHARE = 88
 
 
@@ -36,118 +40,123 @@ def tile_list_ballot_mark_doubts_kernel(
     with ExitStack() as ctx:
         keep = ctx.enter_context(tc.tile_pool(name="keep", bufs=1))
         ring = ctx.enter_context(tc.tile_pool(name="ring", bufs=2))
-        psum = ctx.enter_context(tc.psum_pool(name="psum", bufs=8))
+        psum = ctx.enter_context(tc.psum_pool(name="psum", bufs=1))
 
-        def kept(name, shape, dtype):
-            return keep.tile(shape, dtype, name=name, align_bytes=64)
+        def kept(name, shape, dtype, tag=None):
+            return keep.tile(shape, dtype, name=name, tag=tag or name, align_bytes=64)
 
-        def slab(name, shape):
-            return ring.tile(shape, F32, name=name, tag="slab", bufs=KP * HB, align_bytes=64)
+        def bank(j):
+            return psum.tile([P, BANK], F32, name="bank%d" % j, tag="bank%d" % j)
 
         offs_sb = kept("offs_sb", [P, S // 16], U16)
         offs2_sb = kept("offs2_sb", [P, M // 16], U16)
         offs3_sb = kept("offs3_sb", [P, M // 16], U16)
         tab_sb = [kept("tab%d" % a, [P, T], U32) for a in range(KP)]
         tabs_sb = kept("tabs_sb", [P, T], U8)
-        w4_raw = kept("w4_raw", [P, HB * 2 * H], U8)
-        w4s_raw = kept("w4s_raw", [P, HB * H], U8)
+        w4_sb = kept("w4_sb", [P, HB * 2 * H], U8)
+        w4s_sb = kept("w4s_sb", [P, HB * H], U8)
         gain_sb = kept("gain_sb", [P, HB, PACK], F32)
         clear_sb = kept("clear_sb", [P, HB, PACK], F32)
         wgt_sb = kept("wgt_sb", [P, M], F32)
         wgo_sb = kept("wgo_sb", [P, M], F32)
-        blank_sb = [kept("blank%d" % b, [P, PACK, M], F32) for b in range(HB)]
+        wgo_t = kept("wgo_t", [P, M_BLOCKS * GROUPS], F32)
+        ident = kept("ident", [P, P], F32)
         pages = [kept("page%d" % j, [P, T2], F32) for j in range(PAGES)]
+        late = kept("late", [P, (PACK + 1) * HALF], F32)
+        z_late = late[:, : PACK * HALF]
         warm = kept("warm", [P, 2], F32)
 
         nc.vector.memset(tabs_sb[:].bitcast(I32), 0)
-        nc.vector.memset(w4s_raw[:].bitcast(I32), 0)
+        nc.vector.memset(w4s_sb[:].bitcast(I32), 0)
         nc.vector.memset(warm[:, 0:1], 1.0)
         nc.scalar.activation(out=warm[:, 1:2], in_=warm[:, 0:1], func=ACT.Abs_reciprocal_sqrt)
         for page in pages:
             nc.vector.memset(page[:], 0.0)
-
-        tabs32 = tab_scales.bitcast(I32)
-        w4s32 = w4_scales.bitcast(I32)
-
-        def load_tab_scales():
-            for q in range(4):
-                nc.sync.dma_start(
-                    out=tabs_sb[32 * q : 32 * q + 4 * KP, :].bitcast(I32), in_=tabs32[:, 4 * q : 4 * q + 4, :]
-                )
-
-        def load_w4_scales():
-            for q in range(4):
-                nc.sync.dma_start(
-                    out=w4s_raw[32 * q : 32 * q + 4, :].bitcast(I32).rearrange("r (a n) -> r a n", a=HB),
-                    in_=w4s32[:, 4 * q : 4 * q + 4, :].rearrange("a r n -> r a n"),
-                )
-
-        def load_rows_vector(dst, vec):
-            nc.sync.dma_start(out=dst[:], in_=vec.rearrange("(b p i) -> p b i", b=HB, i=PACK))
+        make_identity(nc, ident[:])
 
         raw = {}
+        blank_pairs = {}
 
         def load_tab(a):
             nc.sync.dma_start(
                 out=tab_sb[a][:].bitcast(I32), in_=tab_words[a].rearrange("p n t -> p (n t)").bitcast(I32)
             )
 
+        def load_tab_scales():
+            for q in range(4):
+                nc.sync.dma_start(
+                    out=tabs_sb[32 * q : 32 * q + 4 * KP, :].bitcast(I32),
+                    in_=tab_scales.bitcast(I32)[:, 4 * q : 4 * q + 4, :],
+                )
+
+        def load_w4():
+            nc.sync.dma_start(
+                out=w4_sb[:].bitcast(I32).rearrange("p (a n) -> p a n", a=HB),
+                in_=w4_words.bitcast(I32).rearrange("a p n -> p a n"),
+            )
+            for q in range(4):
+                nc.sync.dma_start(
+                    out=w4s_sb[32 * q : 32 * q + 4, :].bitcast(I32).rearrange("r (a n) -> r a n", a=HB),
+                    in_=w4_scales.bitcast(I32)[:, 4 * q : 4 * q + 4, :].rearrange("a r n -> r a n"),
+                )
+
+        def load_row_factors(dst, vec):
+            nc.sync.dma_start(out=dst[:], in_=vec.rearrange("(b p i) -> p b i", b=HB, i=PACK))
+
         def load_w1(a, b):
-            raw[a, b] = slab("raw%d%d" % (a, b), [P, PACK, SPAN])
+            raw[a, b] = kept("raw%d%d" % (a, b), [P, PACK, SPAN], F32)
             rows = w1[a * SPAN : (a + 1) * SPAN, b * SPAN : (b + 1) * SPAN]
             nc.sync.dma_start(out=raw[a, b][:], in_=rows.rearrange("(p j) c -> p j c", j=PACK))
 
-        def load_blank(b):
-            rows = blank[b * SPAN : (b + 1) * SPAN, :]
-            nc.sync.dma_start(out=blank_sb[b][:], in_=rows.rearrange("(p i) m -> p i m", i=PACK))
+        def load_blank(b, m0, width, pair):
+            rows = blank[b * SPAN : (b + 1) * SPAN, m0 : m0 + width].rearrange("(p i) m -> p i m", i=PACK)
+            if (b, m0, pair) == (1, 0, 1):
+                dst = z_late[:, : 2 * HALF]
+            else:
+                dst = kept("blank%d_%d_%d" % (b, m0, pair), [P, 2 * width], F32)[:]
+            nc.sync.dma_start(out=dst.rearrange("p (i m) -> p i m", i=2), in_=rows[:, 2 * pair : 2 * pair + 2, :])
+            blank_pairs.setdefault((b, m0), []).append(dst)
 
         load_tab(0)
-        load_tab_scales()
         nc.sync.dma_start(out=offs_sb[:], in_=offs)
-        nc.sync.dma_start(
-            out=w4_raw[:].bitcast(I32).rearrange("p (a n) -> p a n", a=HB),
-            in_=w4_words.bitcast(I32).rearrange("a p n -> p a n"),
-        )
+        load_tab_scales()
         load_w1(0, 0)
         load_tab(1)
         load_w1(1, 0)
-        load_w4_scales()
-        load_rows_vector(gain_sb, gain)
+        load_row_factors(gain_sb, gain)
         load_tab(2)
         load_w1(2, 0)
         nc.sync.dma_start(out=offs2_sb[:], in_=offs2)
         nc.sync.dma_start(out=wgt_sb[:], in_=wgt)
-        load_blank(0)
-        for a in range(KP):
-            load_w1(a, 1)
-        load_rows_vector(clear_sb, clear)
-        load_blank(1)
-        nc.sync.dma_start(out=offs3_sb[:], in_=offs3)
+        load_w1(0, 1)
+        load_w1(1, 1)
+        load_blank(0, 0, M, 0)
+        load_w1(2, 1)
+        load_row_factors(clear_sb, clear)
+        load_blank(0, 0, M, 1)
+        for m0 in (0, HALF):
+            for pair in range(2):
+                load_blank(1, m0, HALF, pair)
         nc.sync.dma_start(out=wgo_sb[:], in_=wgo)
+        load_w4()
+        nc.sync.dma_start(out=offs3_sb[:], in_=offs3)
 
         v_codes = [kept("v_codes%d" % a, [P, S], U32) for a in range(KP)]
         v_scales = kept("v_scales", [P, S], U8)
         w1_codes = {(a, b): kept("w1c%d%d" % (a, b), [P, SPAN], U32) for a in range(KP) for b in range(HB)}
         w1_scales = {(a, b): kept("w1s%d%d" % (a, b), [P, SPAN], U8) for a in range(KP) for b in range(HB)}
-        w4_codes = kept("w4_codes", [P, HB * 2 * H], U8)
-        w4_sc = kept("w4_sc", [P, HB * H], U8)
+
+        stage = kept("stage", [P, T], F32, tag="tab1")
 
         def gather_tab(a):
             nc.vector.tensor_copy(out=v_codes[a][:], in_=tab_sb[a][:].indirect(offs_sb[:]))
 
-        def deal_w4():
-            nc.vector.tensor_copy(
-                out=w4_codes[:].rearrange("p (g i q e) -> p g q i e", i=PACK, q=P, e=2),
-                in_=w4_raw[:].rearrange("p (g q i e) -> p g q i e", i=PACK, q=P, e=2),
-            )
-            nc.vector.tensor_copy(
-                out=w4_sc[:].rearrange("p (g i q) -> p g q i", i=PACK, q=P),
-                in_=w4s_raw[:].rearrange("p (g q i) -> p g q i", i=PACK, q=P),
-            )
-
         def quantize_w1(a, b, vec_cols, pieces):
-            grouped = ring.tile([P, PACK * SPAN], BF16, name="grouped", align_bytes=64)
-            dst = grouped[:].rearrange("p (t q j) -> p q j t", t=PACK, j=PACK)
+            if b == 0:
+                grouped = ring.tile([P, PACK * SPAN], BF16, name="grouped", align_bytes=64)[:]
+            else:
+                grouped = stage[:, a * 2 * M : (a + 1) * 2 * M].bitcast(BF16)
+            dst = grouped.rearrange("p (t q j) -> p q j t", t=PACK, j=PACK)
             src = raw[a, b][:].rearrange("p j (q t) -> p q j t", t=PACK)
             if vec_cols > 0:
                 nc.vector.tensor_copy(out=dst[:, :vec_cols], in_=src[:, :vec_cols])
@@ -163,12 +172,12 @@ def tile_list_ballot_mark_doubts_kernel(
 
         h_sb = {}
 
-        def first_product(b):
-            for i in range(PACK):
+        def first_product(b, tiles):
+            for i in tiles:
                 h_sb[b, i] = ring.tile([P, S], F32, name="h_sb", bufs=4, align_bytes=64)
                 cols = slice(i * P, (i + 1) * P)
                 for s in range(0, S, BANK):
-                    acc = psum.tile([P, BANK], F32, name="acc")
+                    acc = bank(2 * i + s // BANK)
                     for a in range(KP):
                         nc.tensor.matmul_mx(
                             out=acc[:],
@@ -185,72 +194,126 @@ def tile_list_ballot_mark_doubts_kernel(
 
         z_codes = [kept("z_codes%d" % b, [P, M], U32) for b in range(HB)]
         z_scales = [kept("z_scales%d" % b, [P, M], U8) for b in range(HB)]
-        z_sb = {}
+        z_parts = {
+            (0, 0): (kept("z0", [P, PACK * M], F32, tag="raw00")[:], M),
+            (1, 0): (kept("z1", [P, PACK * HALF], F32, tag="raw10")[:], HALF),
+            (1, HALF): (z_late, HALF),
+        }
+
+        x0_slots = stage[:].rearrange("p (r m) -> p r m", m=M)
+        x0_pairs = (x0_slots[:, 6:8, :], x0_slots[:, 1:6:4, :])
+
+        def picked(b, m0, pair):
+            z, width = z_parts[b, m0]
+            if b == 0:
+                return x0_pairs[pair]
+            return z[:, 2 * pair * width : 2 * (pair + 1) * width].rearrange("p (r m) -> p r m", r=2)
 
         def entries(lists, m0, width):
             return lists[:, m0 // 16 : (m0 + width) // 16]
 
-        def make_z(b, m0, width):
-            z = slab("z%d_%d" % (b, m0), [P, PACK, width])
-            z_sb[b, m0] = z
-            cols = slice(m0, m0 + width)
-            for i in range(PACK + 1):
-                if i < PACK:
-                    nc.vector.tensor_tensor(
-                        out=z[:, i, :], in0=h_sb[b, i][:].indirect(entries(offs2_sb, m0, width)), in1=wgt_sb[:, cols], op=MULT
-                    )
-                if i > 0:
-                    nc.vector.tensor_tensor(
-                        out=z[:, i - 1, :], in0=z[:, i - 1, :], in1=blank_sb[b][:, i - 1, cols], op=SUB
-                    )
+        def gather_z(b, m0, tiles):
+            z, width = z_parts[b, m0]
+            for i in tiles:
+                nc.vector.tensor_tensor(
+                    out=picked(b, m0, i // 2)[:, i % 2, :],
+                    in0=h_sb[b, i][:].indirect(entries(offs2_sb, m0, width)),
+                    in1=wgt_sb[:, m0 : m0 + width],
+                    op=MULT,
+                )
 
-        def quantize_z(b, m0, width):
-            zq = ring.tile([P, PACK * width], BF16, name="zq", align_bytes=64)
+        def subtract_blank(b, m0, pair):
+            z, width = z_parts[b, m0]
+            nc.vector.tensor_tensor(
+                out=z[:, 2 * pair * width : 2 * (pair + 1) * width].rearrange("p (r m) -> p r m", r=2),
+                in0=picked(b, m0, pair),
+                in1=blank_pairs[b, m0][pair].rearrange("p (r m) -> p r m", r=2),
+                op=SUB,
+            )
+
+        def make_z(b, m0):
+            gather_z(b, m0, (0, 1, 2))
+            subtract_blank(b, m0, 0)
+            gather_z(b, m0, (3,))
+            subtract_blank(b, m0, 1)
+
+        def quantize_z(b, m0):
+            z0 = m0 if (b, m0) in z_parts else 0
+            z, width = z_parts[b, z0]
+            src = z.rearrange("p (i m) -> p i m", i=PACK)[:, :, m0 - z0 : m0 - z0 + HALF]
+            if (b, m0) == (1, 0):
+                zq = z_late[:, 1 * HALF : 3 * HALF].bitcast(BF16)
+            elif (b, m0) == (0, 0):
+                zq = late[:, 3 * HALF :].bitcast(BF16)
+            else:
+                zq = ring.tile([P, PACK * HALF], BF16, name="zq", align_bytes=64)[:]
             nc.scalar.copy(
-                out=zq[:].rearrange("p (c k i) -> p c i k", k=4, i=PACK),
-                in_=z_sb[b, m0][:].rearrange("p i (c k) -> p c i k", k=4),
+                out=zq.rearrange("p (c k i) -> p c i k", k=4, i=PACK),
+                in_=src.rearrange("p i (c k) -> p c i k", k=4),
             )
             nc.vector.quantize_mx(
-                out=z_codes[b][:, m0 : m0 + width].bitcast(E4M3X4), scales=z_scales[b][:, m0 : m0 + width], in_=zq[:]
+                out=z_codes[b][:, m0 : m0 + HALF].bitcast(E4M3X4), scales=z_scales[b][:, m0 : m0 + HALF], in_=zq
             )
 
-        damp = {}
+        damp = [kept("damp%d" % b, [P, PACK * M], F32, tag="raw%d1" % b) for b in range(HB)]
+        e_t = kept("e_t", [P, M_BLOCKS * H], F32, tag="tab0")
 
-        def make_damp(b, i, m0, width):
-            r = damp[b][:, i, m0 : m0 + width]
-            for (zb, z0), z in z_sb.items():
-                lo, hi = max(m0, z0), min(m0 + width, z0 + z.shape[2])
-                if zb == b and lo < hi:
-                    nc.scalar.activation(
-                        out=damp[b][:, i, lo:hi], in_=z[:, i, lo - z0 : hi - z0], func=ACT.Abs, scale=clear_sb[:, b, i : i + 1]
-                    )
+        def turn_wgo():
+            acc = bank(7)
+            for mb in range(M_BLOCKS):
+                nc.tensor.transpose(acc[:, mb * P : (mb + 1) * P], wgo_sb[:, mb * P : (mb + 1) * P], ident[:])
+            nc.scalar.copy(out=wgo_t[:], in_=acc[:, ::GROUP_ROWS])
+
+        def z_half(b, m0):
+            z0 = m0 if (b, m0) in z_parts else 0
+            z, width = z_parts[b, z0]
+            return z.rearrange("p (i m) -> p i m", i=PACK)[:, :, m0 - z0 : m0 - z0 + HALF]
+
+        def make_damp(n, m0):
+            b, i = divmod(n, PACK)
+            r = damp[b][:, i * M + m0 : i * M + m0 + HALF]
+            nc.scalar.activation(out=r, in_=z_half(b, m0)[:, i, :], func=ACT.Abs, scale=clear_sb[:, b, i : i + 1])
             nc.scalar.activation(out=r, in_=r, func=ACT.Abs_reciprocal_sqrt, bias=1.0)
             nc.scalar.activation(out=r, in_=r, func=ACT.Square)
 
-        def make_y(b, i, m0, width):
-            acc = psum.tile([P, BANK], F32, name="acc")
-            step = BANK if width == BANK else P
-            for c in range(0, width, step):
+        def second_product(b, m0):
+            for mb in range(m0 // P, (m0 + HALF) // P):
+                acc = bank(mb % 2)
                 for a in range(HB):
-                    col = (a * HB + b) * SPAN + i * P
+                    col = a * H + b * SPAN
                     nc.tensor.matmul_mx(
-                        out=acc[:, c : c + step],
-                        lhsT=w4_codes[:, 2 * col : 2 * (col + P)].bitcast(E2M1X4),
-                        lhsT_scale=w4_sc[:, col : col + P],
-                        rhs=z_codes[a][:, m0 + c : m0 + c + step].bitcast(E4M3X4),
-                        rhs_scale=z_scales[a][:, m0 + c : m0 + c + step],
+                        out=acc[:],
+                        lhsT=z_codes[a][:, mb * P : (mb + 1) * P].bitcast(E4M3X4),
+                        lhsT_scale=z_scales[a][:, mb * P : (mb + 1) * P],
+                        rhs=w4_sb[:, 2 * col : 2 * (col + SPAN)].bitcast(E2M1X4),
+                        rhs_scale=w4s_sb[:, col : col + SPAN],
                         start=(a == 0),
                         stop=(a == HB - 1),
                     )
-            make_damp(b, i, m0, width)
-            y = ring.tile([P, M], F32, name="y", bufs=3, align_bytes=64)
-            nc.vector.tensor_tensor(out=y[:, :width], in0=acc[:, :width], in1=damp[b][:, i, m0 : m0 + width], op=MULT)
-            return y
+                block = e_t[:, (mb * HB + b) * SPAN : (mb * HB + b + 1) * SPAN].rearrange("p (i q) -> p i q", i=PACK)
+                for g in range(GROUPS):
+                    run = PACK * GROUP_ROWS
+                    nc.scalar.activation(
+                        out=block[:, :, g * GROUP_ROWS : (g + 1) * GROUP_ROWS],
+                        in_=acc[:, g * run : (g + 1) * run].rearrange("p (q i) -> p i q", i=PACK),
+                        func=ACT.Copy,
+                        scale=wgo_t[:, mb * GROUPS + g : mb * GROUPS + g + 1],
+                    )
 
-        def place(y, b, i, m0, width):
-            page = pages[(b * PACK + i) % PAGES]
+        def place(n, m0, width=HALF):
+            b, i = divmod(n, PACK)
+            acc = bank(4 + n % 4)
+            for mb in range(m0 // P, (m0 + width) // P):
+                col = ((mb * HB + b) * PACK + i) * P
+                nc.tensor.transpose(acc[:, mb * P - m0 : (mb + 1) * P - m0], e_t[:, col : col + P], ident[:])
+            e = ring.tile([P, HALF], F32, name="e", bufs=4, align_bytes=64)
+            nc.scalar.copy(out=e[:, :width], in_=acc[:, :width])
+            page = pages[n % PAGES]
             nc.vector.tensor_tensor(
-                out=page[:].indirect(entries(offs3_sb, m0, width)), in0=y[:, :width], in1=wgo_sb[:, m0 : m0 + width], op=MULT
+                out=page[:].indirect(entries(offs3_sb, m0, width)),
+                in0=e[:, :width],
+                in1=damp[b][:, i * M + m0 : i * M + m0 + width],
+                op=MULT,
             )
             if m0 + width == M:
                 rows = out[b * SPAN : (b + 1) * SPAN, :].rearrange("(p i) n -> p i n", i=PACK)
@@ -259,30 +322,51 @@ def tile_list_ballot_mark_doubts_kernel(
         gather_tab(0)
         nc.vector.tensor_copy(out=v_scales[:], in_=tabs_sb[:].indirect(offs_sb[:]))
         quantize_w1(0, 0, 0, 1)
-        deal_w4()
         gather_tab(1)
         quantize_w1(1, 0, 0, 1)
         gather_tab(2)
         quantize_w1(2, 0, VEC_SHARE, PACK)
-        first_product(0)
-        make_z(0, 0, M)
+        first_product(0, (0, 1, 2))
+        gather_z(0, 0, (0, 1))
         quantize_w1(0, 1, 0, 1)
-        quantize_w1(1, 1, 0, 1)
-        quantize_w1(2, 1, P, PACK)
-        quantize_z(0, 0, M)
-        first_product(1)
-        make_z(1, 0, HALF)
-        quantize_z(1, 0, HALF)
-        make_z(1, HALF, HALF)
-        quantize_z(1, HALF, HALF)
-
-        for b in range(HB):
-            damp[b] = slab("damp%d" % b, [P, PACK, M])
-        steps = [(0, i, m0, HALF) for m0 in (0, HALF) for i in range(SPLIT_TILES)]
-        steps = steps + [(n // PACK, n % PACK, 0, M) for n in range(SPLIT_TILES, HB * PACK)]
-        ahead = make_y(*steps[0])
-        for n, step in enumerate(steps):
-            y = ahead
-            if n + 1 < len(steps):
-                ahead = make_y(*steps[n + 1])
-            place(y, *step)
+        quantize_w1(1, 1, P, 1)
+        first_product(0, (3,))
+        subtract_blank(0, 0, 0)
+        gather_z(0, 0, (2,))
+        quantize_w1(2, 1, 0, PACK)
+        gather_z(0, 0, (3,))
+        first_product(1, range(PACK))
+        subtract_blank(0, 0, 1)
+        make_damp(0, 0)
+        make_damp(1, 0)
+        quantize_z(0, 0)
+        make_z(1, 0)
+        turn_wgo()
+        quantize_z(1, 0)
+        make_z(1, HALF)
+        second_product(0, 0)
+        place(0, 0)
+        place(1, 0)
+        for n in (2, 3):
+            make_damp(n, 0)
+            place(n, 0)
+        second_product(1, 0)
+        make_damp(4, 0)
+        place(4, 0)
+        quantize_z(0, HALF)
+        make_damp(5, 0)
+        place(5, 0)
+        quantize_z(1, HALF)
+        make_damp(6, 0)
+        place(6, 0)
+        make_damp(7, 0)
+        place(7, 0)
+        second_product(0, HALF)
+        for n in range(PACK):
+            make_damp(n, HALF)
+            place(n, HALF)
+            if n == 3:
+                second_product(1, HALF)
+        for n in range(PACK, HB * PACK):
+            make_damp(n, HALF)
+            place(n, HALF)

@@ -62,7 +62,7 @@ def tile_list_ballot_mark_doubts_kernel(
         wgo_t = kept("wgo_t", [P, M_BLOCKS * GROUPS], F32)
         ident = kept("ident", [P, P], F32)
         pages = [kept("page%d" % j, [P, T2], F32) for j in range(PAGES)]
-        late = kept("late", [P, (PACK + 1) * HALF], F32)
+        late = kept("late", [P, (PACK + 3) * HALF], F32)
         z_late = late[:, : PACK * HALF]
         warm = kept("warm", [P, 2], F32)
 
@@ -123,9 +123,9 @@ def tile_list_ballot_mark_doubts_kernel(
         load_w1(0, 0)
         load_tab(1)
         load_w1(1, 0)
-        load_row_factors(gain_sb, gain)
         load_tab(2)
         load_w1(2, 0)
+        load_row_factors(gain_sb, gain)
         nc.sync.dma_start(out=offs2_sb[:], in_=offs2)
         nc.sync.dma_start(out=wgt_sb[:], in_=wgt)
         load_w1(0, 1)
@@ -237,22 +237,17 @@ def tile_list_ballot_mark_doubts_kernel(
             gather_z(b, m0, (3,))
             subtract_blank(b, m0, 1)
 
-        def quantize_z(b, m0):
-            z0 = m0 if (b, m0) in z_parts else 0
-            z, width = z_parts[b, z0]
-            src = z.rearrange("p (i m) -> p i m", i=PACK)[:, :, m0 - z0 : m0 - z0 + HALF]
-            if (b, m0) == (1, 0):
-                zq = z_late[:, 1 * HALF : 3 * HALF].bitcast(BF16)
-            elif (b, m0) == (0, 0):
-                zq = late[:, 3 * HALF :].bitcast(BF16)
-            else:
-                zq = ring.tile([P, PACK * HALF], BF16, name="zq", align_bytes=64)[:]
+        def quantize_z(b, m0, width, staging):
+            z0 = HALF if (b, m0 >= HALF) == (1, True) else 0
+            z, part = z_parts[b, z0]
+            src = z.rearrange("p (i m) -> p i m", i=PACK)[:, :, m0 - z0 : m0 - z0 + width]
+            zq = staging.bitcast(BF16)
             nc.scalar.copy(
                 out=zq.rearrange("p (c k i) -> p c i k", k=4, i=PACK),
                 in_=src.rearrange("p i (c k) -> p c i k", k=4),
             )
             nc.vector.quantize_mx(
-                out=z_codes[b][:, m0 : m0 + HALF].bitcast(E4M3X4), scales=z_scales[b][:, m0 : m0 + HALF], in_=zq
+                out=z_codes[b][:, m0 : m0 + width].bitcast(E4M3X4), scales=z_scales[b][:, m0 : m0 + width], in_=zq
             )
 
         damp = [kept("damp%d" % b, [P, PACK * M], F32, tag="raw%d1" % b) for b in range(HB)]
@@ -269,15 +264,26 @@ def tile_list_ballot_mark_doubts_kernel(
             z, width = z_parts[b, z0]
             return z.rearrange("p (i m) -> p i m", i=PACK)[:, :, m0 - z0 : m0 - z0 + HALF]
 
+        def damp_rows(n, m0, rows):
+            b, i = divmod(n, PACK)
+            first = (m0 // HALF * PACK + i) * HALF
+            return damp[b][:, first : first + rows * HALF]
+
         def make_damp(n, m0):
             b, i = divmod(n, PACK)
-            r = damp[b][:, i * M + m0 : i * M + m0 + HALF]
-            nc.scalar.activation(out=r, in_=z_half(b, m0)[:, i, :], func=ACT.Abs, scale=clear_sb[:, b, i : i + 1])
+            for j in range(2):
+                nc.scalar.activation(
+                    out=damp_rows(n + j, m0, 1),
+                    in_=z_half(b, m0)[:, i + j, :],
+                    func=ACT.Abs,
+                    scale=clear_sb[:, b, i + j : i + j + 1],
+                )
+            r = damp_rows(n, m0, 2)
             nc.scalar.activation(out=r, in_=r, func=ACT.Abs_reciprocal_sqrt, bias=1.0)
             nc.scalar.activation(out=r, in_=r, func=ACT.Square)
 
-        def second_product(b, m0):
-            for mb in range(m0 // P, (m0 + HALF) // P):
+        def second_product(b, m0, width=HALF):
+            for mb in range(m0 // P, (m0 + width) // P):
                 acc = bank(mb % 2)
                 for a in range(HB):
                     col = a * H + b * SPAN
@@ -300,24 +306,29 @@ def tile_list_ballot_mark_doubts_kernel(
                         scale=wgo_t[:, mb * GROUPS + g : mb * GROUPS + g + 1],
                     )
 
-        def place(n, m0, width=HALF):
-            b, i = divmod(n, PACK)
-            acc = bank(4 + n % 4)
-            for mb in range(m0 // P, (m0 + width) // P):
-                col = ((mb * HB + b) * PACK + i) * P
-                nc.tensor.transpose(acc[:, mb * P - m0 : (mb + 1) * P - m0], e_t[:, col : col + P], ident[:])
-            e = ring.tile([P, HALF], F32, name="e", bufs=4, align_bytes=64)
-            nc.scalar.copy(out=e[:, :width], in_=acc[:, :width])
-            page = pages[n % PAGES]
-            nc.vector.tensor_tensor(
-                out=page[:].indirect(entries(offs3_sb, m0, width)),
-                in0=e[:, :width],
-                in1=damp[b][:, i * M + m0 : i * M + m0 + width],
-                op=MULT,
-            )
-            if m0 + width == M:
-                rows = out[b * SPAN : (b + 1) * SPAN, :].rearrange("(p i) n -> p i n", i=PACK)
-                nc.sync.dma_start(out=rows[:, i, :], in_=page[:])
+        placed = []
+
+        def place(tiles, m0, width):
+            acc = bank(4 + len(placed) % 4)
+            placed.append(tiles)
+            for j, n in enumerate(tiles):
+                b, i = divmod(n, PACK)
+                for c in range(0, width, P):
+                    col = (((m0 + c) // P * HB + b) * PACK + i) * P
+                    nc.tensor.transpose(acc[:, j * width + c : j * width + c + P], e_t[:, col : col + P], ident[:])
+            e = ring.tile([P, BANK], F32, name="e", bufs=3, align_bytes=64)
+            nc.scalar.copy(out=e[:], in_=acc[:])
+            for j, n in enumerate(tiles):
+                b, i = divmod(n, PACK)
+                nc.vector.tensor_tensor(
+                    out=pages[n][:].indirect(entries(offs3_sb, m0, width)),
+                    in0=e[:, j * width : (j + 1) * width],
+                    in1=damp_rows(n, m0, 1)[:, m0 % HALF : m0 % HALF + width],
+                    op=MULT,
+                )
+                if m0 + width == M:
+                    rows = out[b * SPAN : (b + 1) * SPAN, :].rearrange("(p i) n -> p i n", i=PACK)
+                    nc.sync.dma_start(out=rows[:, i, :], in_=pages[n][:])
 
         gather_tab(0)
         nc.vector.tensor_copy(out=v_scales[:], in_=tabs_sb[:].indirect(offs_sb[:]))
@@ -328,45 +339,39 @@ def tile_list_ballot_mark_doubts_kernel(
         quantize_w1(2, 0, VEC_SHARE, PACK)
         first_product(0, (0, 1, 2))
         gather_z(0, 0, (0, 1))
-        quantize_w1(0, 1, 0, 1)
-        quantize_w1(1, 1, P, 1)
+        quantize_w1(0, 1, 64, 1)
+        quantize_w1(1, 1, 64, 1)
         first_product(0, (3,))
         subtract_blank(0, 0, 0)
+        quantize_w1(2, 1, 128, PACK)
         gather_z(0, 0, (2,))
-        quantize_w1(2, 1, 0, PACK)
         gather_z(0, 0, (3,))
         first_product(1, range(PACK))
         subtract_blank(0, 0, 1)
         make_damp(0, 0)
-        make_damp(1, 0)
-        quantize_z(0, 0)
+        quantize_z(0, 0, M, late[:, 3 * HALF :])
         make_z(1, 0)
         turn_wgo()
-        quantize_z(1, 0)
+        make_damp(2, 0)
+        quantize_z(1, 0, HALF, late[:, HALF : 3 * HALF])
         make_z(1, HALF)
-        second_product(0, 0)
-        place(0, 0)
-        place(1, 0)
-        for n in (2, 3):
-            make_damp(n, 0)
-            place(n, 0)
+        second_product(0, 0, P)
+        place((0, 1, 2, 3), 0, P)
+        second_product(0, P, P)
+        place((0, 1, 2, 3), P, P)
         second_product(1, 0)
         make_damp(4, 0)
-        place(4, 0)
-        quantize_z(0, HALF)
-        make_damp(5, 0)
-        place(5, 0)
-        quantize_z(1, HALF)
+        place((4, 5), 0, HALF)
+        quantize_z(1, HALF, HALF, late[:, 4 * HALF : 6 * HALF])
         make_damp(6, 0)
-        place(6, 0)
-        make_damp(7, 0)
-        place(7, 0)
+        place((6, 7), 0, HALF)
         second_product(0, HALF)
-        for n in range(PACK):
-            make_damp(n, HALF)
-            place(n, HALF)
-            if n == 3:
-                second_product(1, HALF)
-        for n in range(PACK, HB * PACK):
-            make_damp(n, HALF)
-            place(n, HALF)
+        make_damp(0, HALF)
+        place((0, 1), HALF, HALF)
+        make_damp(2, HALF)
+        place((2, 3), HALF, HALF)
+        second_product(1, HALF)
+        make_damp(4, HALF)
+        place((4, 5), HALF, HALF)
+        make_damp(6, HALF)
+        place((6, 7), HALF, HALF)

@@ -62,8 +62,8 @@ def tile_list_ballot_mark_doubts_kernel(
         wgo_t = kept("wgo_t", [P, M_BLOCKS * GROUPS], F32)
         ident = kept("ident", [P, P], F32)
         pages = [kept("page%d" % j, [P, T2], F32) for j in range(PAGES)]
-        late = kept("late", [P, (PACK + 3) * HALF], F32)
-        z_late = late[:, : PACK * HALF]
+        late = kept("late", [P, (PACK + 2) * HALF], F32)
+        z_late = late[:, HALF : (PACK + 1) * HALF]
         warm = kept("warm", [P, 2], F32)
 
         nc.vector.memset(tabs_sb[:].bitcast(I32), 0)
@@ -111,7 +111,9 @@ def tile_list_ballot_mark_doubts_kernel(
         def load_blank(b, m0, width, pair):
             rows = blank[b * SPAN : (b + 1) * SPAN, m0 : m0 + width].rearrange("(p i) m -> p i m", i=PACK)
             if (b, m0, pair) == (1, 0, 1):
-                dst = z_late[:, : 2 * HALF]
+                dst = late[:, : 2 * HALF]
+            elif (b, m0, pair) == (0, HALF, 1):
+                dst = z_late[:, HALF : 3 * HALF]
             else:
                 dst = kept("blank%d_%d_%d" % (b, m0, pair), [P, 2 * width], F32)[:]
             nc.sync.dma_start(out=dst.rearrange("p (i m) -> p i m", i=2), in_=rows[:, 2 * pair : 2 * pair + 2, :])
@@ -130,13 +132,13 @@ def tile_list_ballot_mark_doubts_kernel(
         nc.sync.dma_start(out=wgt_sb[:], in_=wgt)
         load_w1(0, 1)
         load_w1(1, 1)
-        load_blank(0, 0, M, 0)
+        load_blank(0, 0, HALF, 0)
         load_w1(2, 1)
         load_row_factors(clear_sb, clear)
-        load_blank(0, 0, M, 1)
-        for m0 in (0, HALF):
+        load_blank(0, 0, HALF, 1)
+        for b, m0 in ((1, 0), (0, HALF), (1, HALF)):
             for pair in range(2):
-                load_blank(1, m0, HALF, pair)
+                load_blank(b, m0, HALF, pair)
         nc.sync.dma_start(out=wgo_sb[:], in_=wgo)
         load_w4()
         nc.sync.dma_start(out=offs3_sb[:], in_=offs3)
@@ -195,28 +197,29 @@ def tile_list_ballot_mark_doubts_kernel(
         z_codes = [kept("z_codes%d" % b, [P, M], U32) for b in range(HB)]
         z_scales = [kept("z_scales%d" % b, [P, M], U8) for b in range(HB)]
         z_parts = {
-            (0, 0): (kept("z0", [P, PACK * M], F32, tag="raw00")[:], M),
+            (0, 0): (kept("z0", [P, PACK * HALF], F32, tag="raw00")[:], HALF),
+            (0, HALF): (kept("z0_late", [P, PACK * HALF], F32, tag="raw20")[:], HALF),
             (1, 0): (kept("z1", [P, PACK * HALF], F32, tag="raw10")[:], HALF),
             (1, HALF): (z_late, HALF),
         }
 
         x0_slots = stage[:].rearrange("p (r m) -> p r m", m=M)
-        x0_pairs = (x0_slots[:, 6:8, :], x0_slots[:, 1:6:4, :])
+        x0_pairs = (x0_slots[:, 6:8, :], x0_slots[:, 3:6:2, :])
 
         def picked(b, m0, pair):
             z, width = z_parts[b, m0]
             if b == 0:
-                return x0_pairs[pair]
+                return x0_pairs[pair][:, :, m0 : m0 + width]
             return z[:, 2 * pair * width : 2 * (pair + 1) * width].rearrange("p (r m) -> p r m", r=2)
 
         def entries(lists, m0, width):
             return lists[:, m0 // 16 : (m0 + width) // 16]
 
         def gather_z(b, m0, tiles):
-            z, width = z_parts[b, m0]
+            width = M if b == 0 else HALF
             for i in tiles:
                 nc.vector.tensor_tensor(
-                    out=picked(b, m0, i // 2)[:, i % 2, :],
+                    out=(x0_pairs[i // 2] if b == 0 else picked(b, m0, i // 2))[:, i % 2, :],
                     in0=h_sb[b, i][:].indirect(entries(offs2_sb, m0, width)),
                     in1=wgt_sb[:, m0 : m0 + width],
                     op=MULT,
@@ -238,7 +241,7 @@ def tile_list_ballot_mark_doubts_kernel(
             subtract_blank(b, m0, 1)
 
         def quantize_z(b, m0, width, staging):
-            z0 = HALF if (b, m0 >= HALF) == (1, True) else 0
+            z0 = m0
             z, part = z_parts[b, z0]
             src = z.rearrange("p (i m) -> p i m", i=PACK)[:, :, m0 - z0 : m0 - z0 + width]
             zq = staging.bitcast(BF16)
@@ -343,26 +346,29 @@ def tile_list_ballot_mark_doubts_kernel(
         quantize_w1(1, 1, 64, 1)
         first_product(0, (3,))
         subtract_blank(0, 0, 0)
-        quantize_w1(2, 1, 128, PACK)
+        quantize_w1(2, 1, 128, 2)
         gather_z(0, 0, (2,))
         gather_z(0, 0, (3,))
         first_product(1, range(PACK))
         subtract_blank(0, 0, 1)
         make_damp(0, 0)
-        quantize_z(0, 0, M, late[:, 3 * HALF :])
+        quantize_z(0, 0, HALF, late[:, PACK * HALF :])
         make_z(1, 0)
         turn_wgo()
         make_damp(2, 0)
-        quantize_z(1, 0, HALF, late[:, HALF : 3 * HALF])
+        quantize_z(1, 0, HALF, z_parts[0, HALF][0][:, HALF : 3 * HALF])
+        subtract_blank(0, HALF, 0)
+        subtract_blank(0, HALF, 1)
         make_z(1, HALF)
         second_product(0, 0, P)
         place((0, 1, 2, 3), 0, P)
         second_product(0, P, P)
         place((0, 1, 2, 3), P, P)
+        quantize_z(0, HALF, HALF, kept("zq0", [P, 2 * HALF], F32)[:])
         second_product(1, 0)
+        quantize_z(1, HALF, HALF, kept("zq1", [P, 2 * HALF], F32)[:])
         make_damp(4, 0)
         place((4, 5), 0, HALF)
-        quantize_z(1, HALF, HALF, late[:, 4 * HALF : 6 * HALF])
         make_damp(6, 0)
         place((6, 7), 0, HALF)
         second_product(0, HALF)

from contextlib import ExitStack

import concourse.mybir as mybir
from concourse.masks import make_identity

F32 = mybir.dt.float32
BF16 = mybir.dt.bfloat16
I32 = mybir.dt.int32
U32 = mybir.dt.uint32
U16 = mybir.dt.uint16
U8 = mybir.dt.uint8
E4M3X4 = mybir.dt.float8_e4m3fn_x4
E2M1X4 = mybir.dt.float4_e2m1fn_x4
ACT = mybir.ActivationFunctionType
MULT = mybir.AluOpType.mult
SUB = mybir.AluOpType.subtract

K, H, T, S, M, T2 = 1536, 1024, 4096, 1024, 512, 1024
FLOPS = 2 * K * H * S + 2 * H * H * M

P = 128
PACK = 4
SPAN = P * PACK
KP = K // SPAN
HB = H // SPAN
BANK = 512
HALF = M // 2
GROUPS = 8
GROUP_ROWS = P // GROUPS
M_BLOCKS = M // P
PAGES = 8
SPLIT_TILES = 3
VEC_SHARE = 88


def tile_list_ballot_mark_doubts_kernel(
    tc, tab_words, tab_scales, offs, w1, gain, offs2, wgt, blank, w4_words, w4_scales, clear, offs3, wgo, out
):
    nc = tc.nc
    with ExitStack() as ctx:
        keep = ctx.enter_context(tc.tile_pool(name="keep", bufs=1))
        ring = ctx.enter_context(tc.tile_pool(name="ring", bufs=2))
        psum = ctx.enter_context(tc.psum_pool(name="psum", bufs=1))

        def kept(name, shape, dtype, tag=None):
            return keep.tile(shape, dtype, name=name, tag=tag or name, align_bytes=64)

        def bank(j):
            return psum.tile([P, BANK], F32, name="bank%d" % j, tag="bank%d" % j)

        offs_sb = kept("offs_sb", [P, S // 16], U16)
        offs2_sb = kept("offs2_sb", [P, M // 16], U16)
        offs3_sb = kept("offs3_sb", [P, M // 16], U16)
        tab_sb = [kept("tab%d" % a, [P, T], U32) for a in range(KP)]
        tabs_sb = kept("tabs_sb", [P, T], U8)
        w4_sb = kept("w4_sb", [P, HB * 2 * H], U8)
        w4s_sb = kept("w4s_sb", [P, HB * H], U8)
        gain_sb = kept("gain_sb", [P, HB, PACK], F32)
        clear_sb = kept("clear_sb", [P, HB, PACK], F32)
        wgt_sb = kept("wgt_sb", [P, M], F32)
        wgo_sb = kept("wgo_sb", [P, M], F32)
        wgo_t = kept("wgo_t", [P, M_BLOCKS * GROUPS], F32)
        ident = kept("ident", [P, P], F32)
        pages = [kept("page%d" % j, [P, T2], F32) for j in range(PAGES)]
        late = kept("late", [P, (PACK + 2) * HALF], F32)
        z_late = late[:, HALF : (PACK + 1) * HALF]
        warm = kept("warm", [P, 2], F32)

        nc.vector.memset(tabs_sb[:].bitcast(I32), 0)
        nc.vector.memset(w4s_sb[:].bitcast(I32), 0)
        nc.vector.memset(warm[:, 0:1], 1.0)
        nc.scalar.activation(out=warm[:, 1:2], in_=warm[:, 0:1], func=ACT.Abs_reciprocal_sqrt)
        for page in pages:
            nc.vector.memset(page[:], 0.0)
        make_identity(nc, ident[:])

        raw = {}
        blank_pairs = {}

        def load_tab(a):
            nc.sync.dma_start(
                out=tab_sb[a][:].bitcast(I32), in_=tab_words[a].rearrange("p n t -> p (n t)").bitcast(I32)
            )

        def load_tab_scales():
            for q in range(4):
                nc.sync.dma_start(
                    out=tabs_sb[32 * q : 32 * q + 4 * KP, :].bitcast(I32),
                    in_=tab_scales.bitcast(I32)[:, 4 * q : 4 * q + 4, :],
                )

        def load_w4():
            nc.sync.dma_start(
                out=w4_sb[:].bitcast(I32).rearrange("p (a n) -> p a n", a=HB),
                in_=w4_words.bitcast(I32).rearrange("a p n -> p a n"),
            )
            for q in range(4):
                nc.sync.dma_start(
                    out=w4s_sb[32 * q : 32 * q + 4, :].bitcast(I32).rearrange("r (a n) -> r a n", a=HB),
                    in_=w4_scales.bitcast(I32)[:, 4 * q : 4 * q + 4, :].rearrange("a r n -> r a n"),
                )

        def load_row_factors(dst, vec):
            nc.sync.dma_start(out=dst[:], in_=vec.rearrange("(b p i) -> p b i", b=HB, i=PACK))

        def load_w1(a, b):
            raw[a, b] = kept("raw%d%d" % (a, b), [P, PACK, SPAN], F32)
            rows = w1[a * SPAN : (a + 1) * SPAN, b * SPAN : (b + 1) * SPAN]
            nc.sync.dma_start(out=raw[a, b][:], in_=rows.rearrange("(p j) c -> p j c", j=PACK))

        def load_blank(b, m0, width, pair):
            rows = blank[b * SPAN : (b + 1) * SPAN, m0 : m0 + width].rearrange("(p i) m -> p i m", i=PACK)
            if (b, m0, pair) == (1, 0, 1):
                dst = late[:, : 2 * HALF]
            elif (b, m0, pair) == (0, HALF, 1):
                dst = z_late[:, HALF : 3 * HALF]
            else:
                dst = kept("blank%d_%d_%d" % (b, m0, pair), [P, 2 * width], F32)[:]
            nc.sync.dma_start(out=dst.rearrange("p (i m) -> p i m", i=2), in_=rows[:, 2 * pair : 2 * pair + 2, :])
            blank_pairs.setdefault((b, m0), []).append(dst)

        load_tab(0)
        nc.sync.dma_start(out=offs_sb[:], in_=offs)
        load_tab_scales()
        load_w1(0, 0)
        load_tab(1)
        load_w1(1, 0)
        load_tab(2)
        load_w1(2, 0)
        load_row_factors(gain_sb, gain)
        nc.sync.dma_start(out=offs2_sb[:], in_=offs2)
        nc.sync.dma_start(out=wgt_sb[:], in_=wgt)
        load_w1(0, 1)
        load_w1(1, 1)
        load_blank(0, 0, HALF, 0)
        load_w1(2, 1)
        load_row_factors(clear_sb, clear)
        load_blank(0, 0, HALF, 1)
        for b, m0 in ((1, 0), (0, HALF), (1, HALF)):
            for pair in range(2):
                load_blank(b, m0, HALF, pair)
        nc.sync.dma_start(out=wgo_sb[:], in_=wgo)
        load_w4()
        nc.sync.dma_start(out=offs3_sb[:], in_=offs3)

        v_codes = [kept("v_codes%d" % a, [P, S], U32) for a in range(KP)]
        v_scales = kept("v_scales", [P, S], U8)
        w1_codes = {(a, b): kept("w1c%d%d" % (a, b), [P, SPAN], U32) for a in range(KP) for b in range(HB)}
        w1_scales = {(a, b): kept("w1s%d%d" % (a, b), [P, SPAN], U8) for a in range(KP) for b in range(HB)}

        stage = kept("stage", [P, T], F32, tag="tab1")

        def gather_tab(a):
            nc.vector.tensor_copy(out=v_codes[a][:], in_=tab_sb[a][:].indirect(offs_sb[:]))

        def quantize_w1(a, b, vec_cols, pieces):
            if b == 0:
                grouped = ring.tile([P, PACK * SPAN], BF16, name="grouped", align_bytes=64)[:]
            else:
                grouped = stage[:, a * 2 * M : (a + 1) * 2 * M].bitcast(BF16)
            dst = grouped.rearrange("p (t q j) -> p q j t", t=PACK, j=PACK)
            src = raw[a, b][:].rearrange("p j (q t) -> p q j t", t=PACK)
            if vec_cols > 0:
                nc.vector.tensor_copy(out=dst[:, :vec_cols], in_=src[:, :vec_cols])
            if vec_cols < P:
                nc.scalar.copy(out=dst[:, vec_cols:], in_=src[:, vec_cols:])
            width = SPAN // pieces
            for c in range(0, SPAN, width):
                nc.vector.quantize_mx(
                    out=w1_codes[a, b][:, c : c + width].bitcast(E4M3X4),
                    scales=w1_scales[a, b][:, c : c + width],
                    in_=grouped[:, PACK * c : PACK * (c + width)],
                )

        h_sb = {}

        def first_product(b, tiles):
            for i in tiles:
                h_sb[b, i] = ring.tile([P, S], F32, name="h_sb", bufs=4, align_bytes=64)
                cols = slice(i * P, (i + 1) * P)
                for s in range(0, S, BANK):
                    acc = bank(2 * i + s // BANK)
                    for a in range(KP):
                        nc.tensor.matmul_mx(
                            out=acc[:],
                            lhsT=w1_codes[a, b][:, cols].bitcast(E4M3X4),
                            lhsT_scale=w1_scales[a, b][:, cols],
                            rhs=v_codes[a][:, s : s + BANK].bitcast(E4M3X4),
                            rhs_scale=v_scales[4 * a : P, s : s + BANK],
                            start=(a == 0),
                            stop=(a == KP - 1),
                        )
                    nc.scalar.activation(
                        out=h_sb[b, i][:, s : s + BANK], in_=acc[:], func=ACT.Copy, scale=gain_sb[:, b, i : i + 1]
                    )

        z_codes = [kept("z_codes%d" % b, [P, M], U32) for b in range(HB)]
        z_scales = [kept("z_scales%d" % b, [P, M], U8) for b in range(HB)]
        z_parts = {
            (0, 0): (kept("z0", [P, PACK * HALF], F32, tag="raw00")[:], HALF),
            (0, HALF): (kept("z0_late", [P, PACK * HALF], F32, tag="raw20")[:], HALF),
            (1, 0): (kept("z1", [P, PACK * HALF], F32, tag="raw10")[:], HALF),
            (1, HALF): (z_late, HALF),
        }

        x0_slots = stage[:].rearrange("p (r m) -> p r m", m=M)
        x0_pairs = (x0_slots[:, 6:8, :], x0_slots[:, 3:6:2, :])

        def picked(b, m0, pair):
            z, width = z_parts[b, m0]
            if b == 0:
                return x0_pairs[pair][:, :, m0 : m0 + width]
            return z[:, 2 * pair * width : 2 * (pair + 1) * width].rearrange("p (r m) -> p r m", r=2)

        def entries(lists, m0, width):
            return lists[:, m0 // 16 : (m0 + width) // 16]

        def gather_z(b, m0, tiles):
            width = M if b == 0 else HALF
            for i in tiles:
                nc.vector.tensor_tensor(
                    out=(x0_pairs[i // 2] if b == 0 else picked(b, m0, i // 2))[:, i % 2, :],
                    in0=h_sb[b, i][:].indirect(entries(offs2_sb, m0, width)),
                    in1=wgt_sb[:, m0 : m0 + width],
                    op=MULT,
                )

        def subtract_blank(b, m0, pair):
            z, width = z_parts[b, m0]
            nc.vector.tensor_tensor(
                out=z[:, 2 * pair * width : 2 * (pair + 1) * width].rearrange("p (r m) -> p r m", r=2),
                in0=picked(b, m0, pair),
                in1=blank_pairs[b, m0][pair].rearrange("p (r m) -> p r m", r=2),
                op=SUB,
            )

        def make_z(b, m0):
            gather_z(b, m0, (0, 1, 2))
            subtract_blank(b, m0, 0)
            gather_z(b, m0, (3,))
            subtract_blank(b, m0, 1)

        def quantize_z(b, m0, width, staging):
            z0 = m0
            z, part = z_parts[b, z0]
            src = z.rearrange("p (i m) -> p i m", i=PACK)[:, :, m0 - z0 : m0 - z0 + width]
            zq = staging.bitcast(BF16)
            nc.scalar.copy(
                out=zq.rearrange("p (c k i) -> p c i k", k=4, i=PACK),
                in_=src.rearrange("p i (c k) -> p c i k", k=4),
            )
            nc.vector.quantize_mx(
                out=z_codes[b][:, m0 : m0 + width].bitcast(E4M3X4), scales=z_scales[b][:, m0 : m0 + width], in_=zq
            )

        damp = [kept("damp%d" % b, [P, PACK * M], F32, tag="raw%d1" % b) for b in range(HB)]
        e_t = kept("e_t", [P, M_BLOCKS * H], F32, tag="tab0")

        def turn_wgo():
            acc = bank(7)
            for mb in range(M_BLOCKS):
                nc.tensor.transpose(acc[:, mb * P : (mb + 1) * P], wgo_sb[:, mb * P : (mb + 1) * P], ident[:])
            nc.scalar.copy(out=wgo_t[:], in_=acc[:, ::GROUP_ROWS])

        def z_half(b, m0):
            z0 = m0 if (b, m0) in z_parts else 0
            z, width = z_parts[b, z0]
            return z.rearrange("p (i m) -> p i m", i=PACK)[:, :, m0 - z0 : m0 - z0 + HALF]

        def damp_rows(n, m0, rows):
            b, i = divmod(n, PACK)
            first = (m0 // HALF * PACK + i) * HALF
            return damp[b][:, first : first + rows * HALF]

        def make_damp(n, m0):
            b, i = divmod(n, PACK)
            for j in range(2):
                nc.scalar.activation(
                    out=damp_rows(n + j, m0, 1),
                    in_=z_half(b, m0)[:, i + j, :],
                    func=ACT.Abs,
                    scale=clear_sb[:, b, i + j : i + j + 1],
                )
            r = damp_rows(n, m0, 2)
            nc.scalar.activation(out=r, in_=r, func=ACT.Abs_reciprocal_sqrt, bias=1.0)
            nc.scalar.activation(out=r, in_=r, func=ACT.Square)

        def second_product(b, m0, width=HALF):
            for mb in range(m0 // P, (m0 + width) // P):
                acc = bank(mb % 2)
                for a in range(HB):
                    col = a * H + b * SPAN
                    nc.tensor.matmul_mx(
                        out=acc[:],
                        lhsT=z_codes[a][:, mb * P : (mb + 1) * P].bitcast(E4M3X4),
                        lhsT_scale=z_scales[a][:, mb * P : (mb + 1) * P],
                        rhs=w4_sb[:, 2 * col : 2 * (col + SPAN)].bitcast(E2M1X4),
                        rhs_scale=w4s_sb[:, col : col + SPAN],
                        start=(a == 0),
                        stop=(a == HB - 1),
                    )
                block = e_t[:, (mb * HB + b) * SPAN : (mb * HB + b + 1) * SPAN].rearrange("p (i q) -> p i q", i=PACK)
                for g in range(GROUPS):
                    run = PACK * GROUP_ROWS
                    nc.scalar.activation(
                        out=block[:, :, g * GROUP_ROWS : (g + 1) * GROUP_ROWS],
                        in_=acc[:, g * run : (g + 1) * run].rearrange("p (q i) -> p i q", i=PACK),
                        func=ACT.Copy,
                        scale=wgo_t[:, mb * GROUPS + g : mb * GROUPS + g + 1],
                    )

        placed = []

        def place(tiles, m0, width):
            acc = bank(4 + len(placed) % 4)
            placed.append(tiles)
            for j, n in enumerate(tiles):
                b, i = divmod(n, PACK)
                for c in range(0, width, P):
                    col = (((m0 + c) // P * HB + b) * PACK + i) * P
                    nc.tensor.transpose(acc[:, j * width + c : j * width + c + P], e_t[:, col : col + P], ident[:])
            e = ring.tile([P, BANK], F32, name="e", bufs=3, align_bytes=64)
            nc.scalar.copy(out=e[:], in_=acc[:])
            for j, n in enumerate(tiles):
                b, i = divmod(n, PACK)
                nc.vector.tensor_tensor(
                    out=pages[n][:].indirect(entries(offs3_sb, m0, width)),
                    in0=e[:, j * width : (j + 1) * width],
                    in1=damp_rows(n, m0, 1)[:, m0 % HALF : m0 % HALF + width],
                    op=MULT,
                )
                if m0 + width == M:
                    rows = out[b * SPAN : (b + 1) * SPAN, :].rearrange("(p i) n -> p i n", i=PACK)
                    nc.sync.dma_start(out=rows[:, i, :], in_=pages[n][:])

        gather_tab(0)
        nc.vector.tensor_copy(out=v_scales[:], in_=tabs_sb[:].indirect(offs_sb[:]))
        quantize_w1(0, 0, 0, 1)
        gather_tab(1)
        quantize_w1(1, 0, 0, 1)
        gather_tab(2)
        quantize_w1(2, 0, VEC_SHARE, PACK)
        first_product(0, (0, 1, 2))
        gather_z(0, 0, (0, 1))
        quantize_w1(0, 1, 64, 1)
        quantize_w1(1, 1, 64, 1)
        first_product(0, (3,))
        subtract_blank(0, 0, 0)
        quantize_w1(2, 1, 128, 2)
        gather_z(0, 0, (2,))
        gather_z(0, 0, (3,))
        first_product(1, range(PACK))
        subtract_blank(0, 0, 1)
        make_damp(0, 0)
        quantize_z(0, 0, HALF, late[:, PACK * HALF :])
        make_z(1, 0)
        turn_wgo()
        make_damp(2, 0)
        quantize_z(1, 0, HALF, z_parts[0, HALF][0][:, HALF : 3 * HALF])
        subtract_blank(0, HALF, 0)
        subtract_blank(0, HALF, 1)
        make_z(1, HALF)
        second_product(0, 0, P)
        place((0, 1, 2, 3), 0, P)
        second_product(0, P, P)
        place((0, 1, 2, 3), P, P)
        quantize_z(0, HALF, HALF, kept("zq0", [P, 2 * HALF], F32)[:])
        second_product(1, 0)
        quantize_z(1, HALF, HALF, kept("zq1", [P, 2 * HALF], F32)[:])
        make_damp(4, 0)
        place((4, 5), 0, HALF)
        make_damp(6, 0)
        place((6, 7), 0, HALF)
        second_product(0, HALF)
        make_damp(0, HALF)
        place((0, 1), HALF, HALF)
        make_damp(2, HALF)
        place((2, 3), HALF, HALF)
        second_product(1, HALF)
        make_damp(4, HALF)
        place((4, 5), HALF, HALF)
        make_damp(6, HALF)
        place((6, 7), HALF, HALF)
